import numpy as np
import ml_dtypes


def mxq(x, axis, fmt="e4m3"):
    dtype, down = {"e4m3": (ml_dtypes.float8_e4m3fn, 7), "e5m2": (ml_dtypes.float8_e5m2, 14)}[fmt]
    v = np.moveaxis(np.asarray(x, np.float32).astype(ml_dtypes.bfloat16).astype(np.float64), axis, -1)
    blocks = v.reshape(v.shape[:-1] + (-1, 32))
    amax = np.abs(blocks).max(-1, keepdims=True)
    byte = np.maximum(np.where(amax > 0, np.frexp(amax)[1] - 1 + 127, 0) - down, 1)
    scale = np.exp2(byte - 127.0)
    codes = (blocks / scale).astype(np.float32).astype(dtype).astype(np.float64)
    return np.moveaxis((codes * scale).reshape(v.shape), -1, axis)


WIDE = False


def mx_kscale(k):
    if not WIDE:
        return np.ones(k)
    levels = np.array([10, -10, 5, -5, 0])
    if k % 512:
        return np.exp2(np.random.permutation(np.resize(levels, k // 32))).repeat(32)
    a = np.empty((k // 512, 16))
    for p in range(k // 512):
        a[p, :8] = np.random.permutation(np.resize(levels, 8))
        for g in range(8):
            far = levels[np.abs(levels - a[p, g]) >= 10]
            a[p, g + 8] = far[np.random.randint(len(far))]
    return np.exp2(a.ravel()).repeat(32)


def f64(x):
    return np.asarray(x).astype(np.float64)


def striped(idx):
    return np.tile(np.asarray(idx).reshape(-1, 16).T, (8, 1)).astype(np.uint16)


def unstriped(offs):
    return offs[:16].T.reshape(-1).astype(np.int64)


E2M1 = np.array([0.0, 0.5, 1.0, 1.5, 2.0, 3.0, 4.0, 6.0, -0.0, -0.5, -1.0, -1.5, -2.0, -3.0, -4.0, -6.0])


def pack_weight(w, fmt):
    k, n = w.shape
    w = f64(np.asarray(w, np.float32).astype(ml_dtypes.bfloat16)).reshape(k // 32, 32, n)
    amax = np.abs(w).max(1)
    if fmt == "e4m3":
        byte = np.frexp(amax)[1] - 1 + 127 - 7
    else:
        mant, ex = np.frexp(amax / 6.0)
        byte = np.where(mant > 0.5, ex, ex - 1) + 127
    byte = np.clip(np.where(amax > 0, byte, 1), 1, 254)
    scaled = (w * np.exp2(127.0 - byte)[:, None, :]).reshape(k, n).astype(np.float32)
    by_word = np.ascontiguousarray(scaled.reshape(k // 512, 128, 4, n).transpose(0, 1, 3, 2))
    if fmt == "e4m3":
        words = by_word.astype(ml_dtypes.float8_e4m3fn).view(np.uint8)
    else:
        c = by_word.astype(ml_dtypes.float4_e2m1fn).view(np.uint8) & 0xF
        words = (c[..., 0::2] | (c[..., 1::2] << 4)).reshape(k // 512, 128, 2 * n)
    return np.ascontiguousarray(words), np.ascontiguousarray(byte.astype(np.uint8).reshape(k // 512, 16, n))


def unpack_weight(words, scales, fmt):
    g, _, n = scales.shape
    words = np.ascontiguousarray(words).reshape(g, 128, n, -1)
    if fmt == "e4m3":
        vals = words.view(ml_dtypes.float8_e4m3fn).astype(np.float64)
    else:
        nib = np.empty((g, 128, n, 4), np.uint8)
        nib[..., 0::2] = words & 0xF
        nib[..., 1::2] = words >> 4
        vals = E2M1[nib]
    vals = vals * np.repeat(np.exp2(scales.astype(np.float64) - 127.0), 8, axis=1)[..., None]
    return vals.transpose(0, 1, 3, 2).reshape(g * 512, n)


def sigmoid(v):
    return 1.0 / (1.0 + np.exp(-v))


D, T, I, Q, U, M = 512, 2048, 512, 128, 1024, 2048


def setup_inputs():
    n = np.random.standard_normal
    idx = np.random.permutation(T)[:I]
    idx2 = np.random.permutation(U)[:Q]
    idx3 = np.random.permutation(U)[:Q]
    idx4 = np.random.permutation(M)[:I]
    fd = mx_kscale(D)
    keysp = pack_weight(n((D, T)) / fd[:, None], "e4m3")
    return {
        "users": (n((D, U)) * 1.0 / np.sqrt(D) * fd[:, None]).astype(np.float32),
        "keys_words": keysp[0],
        "keys_scales": keysp[1],
        "old": (np.random.uniform(0.0, 2.0, (Q, M))).astype(np.float32),
        "fade": (np.random.uniform(0.3, 0.9, (Q, 1))).astype(np.float32),
        "offs": striped(idx),
        "offs2": striped(idx2),
        "offs3": striped(idx3),
        "offs4": striped(idx4),
    }


def reference(users, keys_words, keys_scales, old, fade, offs, offs2, offs3, offs4):
    idx = unstriped(offs)
    idx2 = unstriped(offs2)
    idx3 = unstriped(offs3)
    idx4 = unstriped(offs4)
    keysu = unpack_weight(keys_words, keys_scales, "e4m3")
    zq = np.maximum(f64(users)[:, idx2], f64(users)[:, idx3])
    zqq = mxq(zq, 0, "e4m3")
    keysidxg = keysu[:, idx]
    s = zqq.T @ keysidxg
    w = sigmoid(s)
    ws = w * 2.0
    wf = np.zeros((Q, M))
    wf[:, idx4] = ws
    y = f64(old) * f64(fade) + wf
    return y

@@ -1,0 +1,134 @@
+from contextlib import ExitStack
+
+import concourse.mybir as mybir
+
+D, T, I, Q, U, M = 512, 2048, 512, 128, 1024, 2048
+FLOPS = 2 * Q * D * I
+
+F32 = mybir.dt.float32
+BF16 = mybir.dt.bfloat16
+I32 = mybir.dt.int32
+U32 = mybir.dt.uint32
+U16 = mybir.dt.uint16
+U8 = mybir.dt.uint8
+FP8X4 = mybir.dt.float8_e4m3fn_x4
+ALU = mybir.AluOpType
+ACT = mybir.ActivationFunctionType
+
+P = 128
+PACK = 4
+SLOT_CHUNKS = ((0, 256), (256, 256))
+OUT_CHUNK = 512
+
+
+def tile_attend_querylarger_counts_lean_kernel(tc, users, keys_words, keys_scales, old, fade, offs, offs2, offs3, offs4, out):
+    nc = tc.nc
+    with ExitStack() as ctx:
+        lists = ctx.enter_context(tc.tile_pool(name="lists", bufs=1))
+        pool = ctx.enter_context(tc.tile_pool(name="pool", bufs=1))
+        psum = ctx.enter_context(tc.psum_pool(name="psum", bufs=1))
+
+        key_list = lists.tile([P, I // 16], U16, name="key_list")
+        first_list = lists.tile([P, Q // 16], U16, name="first_list")
+        second_list = lists.tile([P, Q // 16], U16, name="second_list")
+        place_list = lists.tile([P, I // 16], U16, name="place_list")
+
+        user_rows = users.rearrange("(p t) u -> p t u", t=PACK)
+        plane0 = pool.tile([P, U], F32, name="plane0", tag="plane0_then_keys")
+        planes12 = pool.tile([P, 2, U], F32, name="planes12", tag="planes12_then_old")
+        plane3 = pool.tile([P, U], F32, name="plane3")
+        nc.sync.dma_start(out=plane0[:], in_=user_rows[:, 0, :])
+        nc.sync.dma_start(first_list[:], offs2)
+        nc.sync.dma_start(second_list[:], offs3)
+        nc.sync.dma_start(key_list[:], offs)
+        nc.sync.dma_start(out=planes12[:], in_=user_rows[:, 1:3, :])
+        nc.sync.dma_start(out=plane3[:], in_=user_rows[:, 3, :])
+        nc.sync.dma_start(place_list[:], offs4)
+        fade_col = pool.tile([P, 1], F32, name="fade_col")
+        nc.sync.dma_start(out=fade_col[:], in_=fade)
+
+        scale_pool = pool.tile([P, T], U8, name="scale_pool", tag="scales_then_first", align_bytes=64)
+        nc.vector.memset(scale_pool[:].bitcast(I32), 0)
+        for quadrant in range(4):
+            nc.scalar.dma_start(
+                out=scale_pool[32 * quadrant : 32 * quadrant + 4, :].bitcast(I32),
+                in_=keys_scales[0, 4 * quadrant : 4 * quadrant + 4, :].bitcast(I32),
+            )
+
+        placed = pool.tile([P, M], F32, name="placed")
+        nc.vector.memset(placed[:], 0.0)
+
+        query = pool.tile([P, Q, PACK], BF16, name="query", align_bytes=64)
+
+        def larger_of(first, second, places):
+            nc.vector.tensor_tensor(
+                query[:, :, places].rearrange("p (c i) t -> p c t i", i=4),
+                first[:].rearrange("p t (c i) -> p c t i", i=4),
+                second[:].rearrange("p t (c i) -> p c t i", i=4),
+                ALU.max,
+            )
+
+        first01 = pool.tile([P, 2, Q], F32, name="first01")
+        second01 = pool.tile([P, 2, Q], F32, name="second01")
+        nc.vector.tensor_copy(first01[:, 0, :], plane0[:].indirect(first_list[:]))
+        nc.vector.tensor_copy(second01[:, 0, :], plane0[:].indirect(second_list[:]))
+
+        word_pool = pool.tile([P, T], I32, name="word_pool", tag="plane0_then_keys")
+        nc.sync.dma_start(out=word_pool[:], in_=keys_words[0].rearrange("p n t -> p (n t)").bitcast(I32))
+
+        key_scales = pool.tile([P, I], U8, name="key_scales", align_bytes=64)
+        nc.vector.tensor_copy(key_scales[:], scale_pool[:].indirect(key_list[:]))
+
+        first23 = pool.tile([P, 2, Q], F32, name="first23", tag="scales_then_first", align_bytes=64)
+        second23 = pool.tile([P, 2, Q], F32, name="second23")
+        nc.vector.tensor_copy(first01[:, 1, :], planes12[:, 0, :].indirect(first_list[:]))
+        nc.scalar.activation(second01[:, 1, :], planes12[:, 0, :].indirect(second_list[:]), ACT.Copy)
+        nc.vector.tensor_copy(first23[:, 0, :], planes12[:, 1, :].indirect(first_list[:]))
+        nc.scalar.activation(second23[:, 0, :], planes12[:, 1, :].indirect(second_list[:]), ACT.Copy)
+        larger_of(first01, second01, slice(0, 2))
+
+        old_sb = pool.tile([P, M], F32, name="old_sb", tag="planes12_then_old")
+        nc.sync.dma_start(out=old_sb[:], in_=old)
+
+        nc.vector.tensor_copy(first23[:, 1, :], plane3[:].indirect(first_list[:]))
+        nc.scalar.activation(second23[:, 1, :], plane3[:].indirect(second_list[:]), ACT.Copy)
+        larger_of(first23, second23, slice(2, 4))
+
+        query_words = pool.tile([P, Q], U32, name="query_words", align_bytes=64)
+        query_scales = pool.tile([P, Q], U8, name="query_scales", align_bytes=64)
+        nc.vector.quantize_mx(
+            out=query_words[:].bitcast(FP8X4),
+            scales=query_scales[:],
+            in_=query[:].rearrange("p q t -> p (q t)"),
+        )
+
+        weights = []
+        for c, (start, width) in enumerate(SLOT_CHUNKS):
+            key_words = pool.tile([P, width], U32, name=f"key_words{c}", align_bytes=64)
+            nc.vector.tensor_copy(
+                key_words[:], word_pool[:].bitcast(U32).indirect(key_list[:, start // 16 : (start + width) // 16])
+            )
+            scores = psum.tile([P, width], F32, name=f"scores{c}")
+            nc.tensor.matmul_mx(
+                out=scores[:],
+                lhsT=query_words[:].bitcast(FP8X4),
+                lhsT_scale=query_scales[:],
+                rhs=key_words[:].bitcast(FP8X4),
+                rhs_scale=key_scales[:, start : start + width],
+                start=True,
+                stop=True,
+            )
+            weight = pool.tile([P, width], F32, name=f"weight{c}")
+            nc.scalar.activation(weight[:], scores[:], ACT.Sigmoid)
+            weights.append(weight)
+
+        for weight, (start, width) in zip(weights, SLOT_CHUNKS):
+            nc.vector.tensor_tensor(
+                placed[:].indirect(place_list[:, start // 16 : (start + width) // 16]), weight[:], weight[:], ALU.add
+            )
+
+        for c in range(M // OUT_CHUNK):
+            cols = slice(c * OUT_CHUNK, (c + 1) * OUT_CHUNK)
+            result = pool.tile([P, OUT_CHUNK], F32, name=f"result{c}")
+            nc.vector.scalar_tensor_tensor(result[:], old_sb[:, cols], fade_col[:], placed[:, cols], ALU.mult, ALU.add)
+            nc.sync.dma_start(out=out[:, cols], in_=result[:])

@@ -17,8 +17,9 @@ ACT = mybir.ActivationFunctionType
 
 P = 128
 PACK = 4
-SLOT_CHUNKS = ((0, 256), (256, 256))
-OUT_CHUNK = 512
+SCORE_CHUNKS = ((0, 128), (128, 256), (384, 128))
+SCATTER_CHUNKS = ((0, 128), (128, 384))
+OUT_CHUNKS = ((0, 256), (256, 512), (768, 512), (1280, 512), (1792, 256))
 
 
 def tile_attend_querylarger_counts_lean_kernel(tc, users, keys_words, keys_scales, old, fade, offs, offs2, offs3, offs4, out):
@@ -33,66 +34,54 @@ def tile_attend_querylarger_counts_lean_kernel(tc, users, keys_words, keys_scale
         second_list = lists.tile([P, Q // 16], U16, name="second_list")
         place_list = lists.tile([P, I // 16], U16, name="place_list")
 
+        warm_in = pool.tile([P, 1], F32, name="warm_in")
+        warm_out = pool.tile([P, 1], F32, name="warm_out")
+        nc.gpsimd.memset(warm_in[:], 0.0)
+        nc.scalar.activation(warm_out[:], warm_in[:], ACT.Sigmoid)
+
+        scale_pool = pool.tile([P, T], U8, name="scale_pool", tag="scales_then_query", align_bytes=64)
+        nc.vector.memset(scale_pool[:, : T // 2].bitcast(I32), 0)
+        nc.gpsimd.memset(scale_pool[:, T // 2 :].bitcast(I32), 0)
+
         user_rows = users.rearrange("(p t) u -> p t u", t=PACK)
-        plane0 = pool.tile([P, U], F32, name="plane0", tag="plane0_then_keys")
-        planes12 = pool.tile([P, 2, U], F32, name="planes12", tag="planes12_then_old")
-        plane3 = pool.tile([P, U], F32, name="plane3")
-        nc.sync.dma_start(out=plane0[:], in_=user_rows[:, 0, :])
+        halves = [pool.tile([P, 2, U], F32, name=f"users{h}") for h in range(2)]
+        nc.sync.dma_start(key_list[:], offs)
+        nc.sync.dma_start(out=halves[0][:], in_=user_rows[:, 0:2, :])
         nc.sync.dma_start(first_list[:], offs2)
         nc.sync.dma_start(second_list[:], offs3)
-        nc.sync.dma_start(key_list[:], offs)
-        nc.sync.dma_start(out=planes12[:], in_=user_rows[:, 1:3, :])
-        nc.sync.dma_start(out=plane3[:], in_=user_rows[:, 3, :])
-        nc.sync.dma_start(place_list[:], offs4)
-        fade_col = pool.tile([P, 1], F32, name="fade_col")
-        nc.sync.dma_start(out=fade_col[:], in_=fade)
-
-        scale_pool = pool.tile([P, T], U8, name="scale_pool", tag="scales_then_first", align_bytes=64)
-        nc.vector.memset(scale_pool[:].bitcast(I32), 0)
         for quadrant in range(4):
-            nc.scalar.dma_start(
+            nc.sync.dma_start(
                 out=scale_pool[32 * quadrant : 32 * quadrant + 4, :].bitcast(I32),
                 in_=keys_scales[0, 4 * quadrant : 4 * quadrant + 4, :].bitcast(I32),
             )
+        nc.sync.dma_start(out=halves[1][:], in_=user_rows[:, 2:4, :])
+        word_pool = pool.tile([P, T], I32, name="word_pool")
+        nc.sync.dma_start(out=word_pool[:], in_=keys_words[0].rearrange("p n t -> p (n t)").bitcast(I32))
+        nc.sync.dma_start(place_list[:], offs4)
+        fade_col = pool.tile([P, 1], F32, name="fade_col")
+        nc.sync.dma_start(out=fade_col[:], in_=fade)
+        old_sb = pool.tile([P, M], F32, name="old_sb")
+        nc.sync.dma_start(out=old_sb[:], in_=old)
 
         placed = pool.tile([P, M], F32, name="placed")
         nc.vector.memset(placed[:], 0.0)
 
-        query = pool.tile([P, Q, PACK], BF16, name="query", align_bytes=64)
-
-        def larger_of(first, second, places):
+        key_scales = pool.tile([P, I], U8, name="key_scales", align_bytes=64)
+        for h in range(2):
+            first = pool.tile([P, 2, Q], F32, name=f"first{h}")
+            second = pool.tile([P, 2, Q], F32, name=f"second{h}")
+            for e in range(2):
+                nc.scalar.activation(first[:, e, :], halves[h][:, e, :].indirect(first_list[:]), ACT.Copy)
+                nc.vector.tensor_copy(second[:, e, :], halves[h][:, e, :].indirect(second_list[:]))
+            if h == 0:
+                nc.vector.tensor_copy(key_scales[:], scale_pool[:].indirect(key_list[:]))
+                query = pool.tile([P, Q, PACK], BF16, name="query", tag="scales_then_query", align_bytes=64)
             nc.vector.tensor_tensor(
-                query[:, :, places].rearrange("p (c i) t -> p c t i", i=4),
+                query[:, :, 2 * h : 2 * h + 2].rearrange("p (c i) t -> p c t i", i=4),
                 first[:].rearrange("p t (c i) -> p c t i", i=4),
                 second[:].rearrange("p t (c i) -> p c t i", i=4),
                 ALU.max,
             )
-
-        first01 = pool.tile([P, 2, Q], F32, name="first01")
-        second01 = pool.tile([P, 2, Q], F32, name="second01")
-        nc.vector.tensor_copy(first01[:, 0, :], plane0[:].indirect(first_list[:]))
-        nc.vector.tensor_copy(second01[:, 0, :], plane0[:].indirect(second_list[:]))
-
-        word_pool = pool.tile([P, T], I32, name="word_pool", tag="plane0_then_keys")
-        nc.sync.dma_start(out=word_pool[:], in_=keys_words[0].rearrange("p n t -> p (n t)").bitcast(I32))
-
-        key_scales = pool.tile([P, I], U8, name="key_scales", align_bytes=64)
-        nc.vector.tensor_copy(key_scales[:], scale_pool[:].indirect(key_list[:]))
-
-        first23 = pool.tile([P, 2, Q], F32, name="first23", tag="scales_then_first", align_bytes=64)
-        second23 = pool.tile([P, 2, Q], F32, name="second23")
-        nc.vector.tensor_copy(first01[:, 1, :], planes12[:, 0, :].indirect(first_list[:]))
-        nc.scalar.activation(second01[:, 1, :], planes12[:, 0, :].indirect(second_list[:]), ACT.Copy)
-        nc.vector.tensor_copy(first23[:, 0, :], planes12[:, 1, :].indirect(first_list[:]))
-        nc.scalar.activation(second23[:, 0, :], planes12[:, 1, :].indirect(second_list[:]), ACT.Copy)
-        larger_of(first01, second01, slice(0, 2))
-
-        old_sb = pool.tile([P, M], F32, name="old_sb", tag="planes12_then_old")
-        nc.sync.dma_start(out=old_sb[:], in_=old)
-
-        nc.vector.tensor_copy(first23[:, 1, :], plane3[:].indirect(first_list[:]))
-        nc.scalar.activation(second23[:, 1, :], plane3[:].indirect(second_list[:]), ACT.Copy)
-        larger_of(first23, second23, slice(2, 4))
 
         query_words = pool.tile([P, Q], U32, name="query_words", align_bytes=64)
         query_scales = pool.tile([P, Q], U8, name="query_scales", align_bytes=64)
@@ -102,8 +91,8 @@ def tile_attend_querylarger_counts_lean_kernel(tc, users, keys_words, keys_scale
             in_=query[:].rearrange("p q t -> p (q t)"),
         )
 
-        weights = []
-        for c, (start, width) in enumerate(SLOT_CHUNKS):
+        weight = pool.tile([P, I], F32, name="weight")
+        for c, (start, width) in enumerate(SCORE_CHUNKS):
             key_words = pool.tile([P, width], U32, name=f"key_words{c}", align_bytes=64)
             nc.vector.tensor_copy(
                 key_words[:], word_pool[:].bitcast(U32).indirect(key_list[:, start // 16 : (start + width) // 16])
@@ -118,17 +107,19 @@ def tile_attend_querylarger_counts_lean_kernel(tc, users, keys_words, keys_scale
                 start=True,
                 stop=True,
             )
-            weight = pool.tile([P, width], F32, name=f"weight{c}")
-            nc.scalar.activation(weight[:], scores[:], ACT.Sigmoid)
-            weights.append(weight)
+            nc.scalar.activation(weight[:, start : start + width], scores[:], ACT.Sigmoid)
 
-        for weight, (start, width) in zip(weights, SLOT_CHUNKS):
+        for start, width in SCATTER_CHUNKS:
+            slots = slice(start, start + width)
             nc.vector.tensor_tensor(
-                placed[:].indirect(place_list[:, start // 16 : (start + width) // 16]), weight[:], weight[:], ALU.add
+                placed[:].indirect(place_list[:, start // 16 : (start + width) // 16]),
+                weight[:, slots],
+                weight[:, slots],
+                ALU.add,
             )
 
-        for c in range(M // OUT_CHUNK):
-            cols = slice(c * OUT_CHUNK, (c + 1) * OUT_CHUNK)
-            result = pool.tile([P, OUT_CHUNK], F32, name=f"result{c}")
+        for c, (start, width) in enumerate(OUT_CHUNKS):
+            cols = slice(start, start + width)
+            result = pool.tile([P, width], F32, name=f"result{c}")
             nc.vector.scalar_tensor_tensor(result[:], old_sb[:, cols], fade_col[:], placed[:, cols], ALU.mult, ALU.add)
             nc.sync.dma_start(out=out[:, cols], in_=result[:])

@@ -19,7 +19,7 @@ P = 128
 PACK = 4
 SCORE_CHUNKS = ((0, 128), (128, 256), (384, 128))
 SCATTER_CHUNKS = ((0, 128), (128, 384))
-OUT_CHUNKS = ((0, 256), (256, 512), (768, 512), (1280, 512), (1792, 256))
+OUT_CHUNKS = ((0, 128), (128, 384), (512, 512), (1024, 512), (1536, 384), (1920, 128))
 
 
 def tile_attend_querylarger_counts_lean_kernel(tc, users, keys_words, keys_scales, old, fade, offs, offs2, offs3, offs4, out):

from contextlib import ExitStack

import concourse.mybir as mybir

D, T, I, Q, U, M = 512, 2048, 512, 128, 1024, 2048
FLOPS = 2 * Q * D * I

F32 = mybir.dt.float32
BF16 = mybir.dt.bfloat16
I32 = mybir.dt.int32
U32 = mybir.dt.uint32
U16 = mybir.dt.uint16
U8 = mybir.dt.uint8
FP8X4 = mybir.dt.float8_e4m3fn_x4
ALU = mybir.AluOpType
ACT = mybir.ActivationFunctionType

P = 128
PACK = 4
SCORE_CHUNKS = ((0, 128), (128, 256), (384, 128))
SCATTER_CHUNKS = ((0, 128), (128, 384))
OUT_CHUNKS = ((0, 128), (128, 384), (512, 512), (1024, 512), (1536, 384), (1920, 128))


def tile_attend_querylarger_counts_lean_kernel(tc, users, keys_words, keys_scales, old, fade, offs, offs2, offs3, offs4, out):
    nc = tc.nc
    with ExitStack() as ctx:
        lists = ctx.enter_context(tc.tile_pool(name="lists", bufs=1))
        pool = ctx.enter_context(tc.tile_pool(name="pool", bufs=1))
        psum = ctx.enter_context(tc.psum_pool(name="psum", bufs=1))

        key_list = lists.tile([P, I // 16], U16, name="key_list")
        first_list = lists.tile([P, Q // 16], U16, name="first_list")
        second_list = lists.tile([P, Q // 16], U16, name="second_list")
        place_list = lists.tile([P, I // 16], U16, name="place_list")

        warm_in = pool.tile([P, 1], F32, name="warm_in")
        warm_out = pool.tile([P, 1], F32, name="warm_out")
        nc.gpsimd.memset(warm_in[:], 0.0)
        nc.scalar.activation(warm_out[:], warm_in[:], ACT.Sigmoid)

        scale_pool = pool.tile([P, T], U8, name="scale_pool", tag="scales_then_query", align_bytes=64)
        nc.vector.memset(scale_pool[:, : T // 2].bitcast(I32), 0)
        nc.gpsimd.memset(scale_pool[:, T // 2 :].bitcast(I32), 0)

        user_rows = users.rearrange("(p t) u -> p t u", t=PACK)
        halves = [pool.tile([P, 2, U], F32, name=f"users{h}") for h in range(2)]
        nc.sync.dma_start(key_list[:], offs)
        nc.sync.dma_start(out=halves[0][:], in_=user_rows[:, 0:2, :])
        nc.sync.dma_start(first_list[:], offs2)
        nc.sync.dma_start(second_list[:], offs3)
        for quadrant in range(4):
            nc.sync.dma_start(
                out=scale_pool[32 * quadrant : 32 * quadrant + 4, :].bitcast(I32),
                in_=keys_scales[0, 4 * quadrant : 4 * quadrant + 4, :].bitcast(I32),
            )
        nc.sync.dma_start(out=halves[1][:], in_=user_rows[:, 2:4, :])
        word_pool = pool.tile([P, T], I32, name="word_pool")
        nc.sync.dma_start(out=word_pool[:], in_=keys_words[0].rearrange("p n t -> p (n t)").bitcast(I32))
        nc.sync.dma_start(place_list[:], offs4)
        fade_col = pool.tile([P, 1], F32, name="fade_col")
        nc.sync.dma_start(out=fade_col[:], in_=fade)
        old_sb = pool.tile([P, M], F32, name="old_sb")
        nc.sync.dma_start(out=old_sb[:], in_=old)

        placed = pool.tile([P, M], F32, name="placed")
        nc.vector.memset(placed[:], 0.0)

        key_scales = pool.tile([P, I], U8, name="key_scales", align_bytes=64)
        for h in range(2):
            first = pool.tile([P, 2, Q], F32, name=f"first{h}")
            second = pool.tile([P, 2, Q], F32, name=f"second{h}")
            for e in range(2):
                nc.scalar.activation(first[:, e, :], halves[h][:, e, :].indirect(first_list[:]), ACT.Copy)
                nc.vector.tensor_copy(second[:, e, :], halves[h][:, e, :].indirect(second_list[:]))
            if h == 0:
                nc.vector.tensor_copy(key_scales[:], scale_pool[:].indirect(key_list[:]))
                query = pool.tile([P, Q, PACK], BF16, name="query", tag="scales_then_query", align_bytes=64)
            nc.vector.tensor_tensor(
                query[:, :, 2 * h : 2 * h + 2].rearrange("p (c i) t -> p c t i", i=4),
                first[:].rearrange("p t (c i) -> p c t i", i=4),
                second[:].rearrange("p t (c i) -> p c t i", i=4),
                ALU.max,
            )

        query_words = pool.tile([P, Q], U32, name="query_words", align_bytes=64)
        query_scales = pool.tile([P, Q], U8, name="query_scales", align_bytes=64)
        nc.vector.quantize_mx(
            out=query_words[:].bitcast(FP8X4),
            scales=query_scales[:],
            in_=query[:].rearrange("p q t -> p (q t)"),
        )

        weight = pool.tile([P, I], F32, name="weight")
        for c, (start, width) in enumerate(SCORE_CHUNKS):
            key_words = pool.tile([P, width], U32, name=f"key_words{c}", align_bytes=64)
            nc.vector.tensor_copy(
                key_words[:], word_pool[:].bitcast(U32).indirect(key_list[:, start // 16 : (start + width) // 16])
            )
            scores = psum.tile([P, width], F32, name=f"scores{c}")
            nc.tensor.matmul_mx(
                out=scores[:],
                lhsT=query_words[:].bitcast(FP8X4),
                lhsT_scale=query_scales[:],
                rhs=key_words[:].bitcast(FP8X4),
                rhs_scale=key_scales[:, start : start + width],
                start=True,
                stop=True,
            )
            nc.scalar.activation(weight[:, start : start + width], scores[:], ACT.Sigmoid)

        for start, width in SCATTER_CHUNKS:
            slots = slice(start, start + width)
            nc.vector.tensor_tensor(
                placed[:].indirect(place_list[:, start // 16 : (start + width) // 16]),
                weight[:, slots],
                weight[:, slots],
                ALU.add,
            )

        for c, (start, width) in enumerate(OUT_CHUNKS):
            cols = slice(start, start + width)
            result = pool.tile([P, width], F32, name=f"result{c}")
            nc.vector.scalar_tensor_tensor(result[:], old_sb[:, cols], fade_col[:], placed[:, cols], ALU.mult, ALU.add)
            nc.sync.dma_start(out=out[:, cols], in_=result[:])
